import numpy as np
import ml_dtypes


def mxq(x, axis, fmt="e4m3"):
    dtype, down = {"e4m3": (ml_dtypes.float8_e4m3fn, 7), "e5m2": (ml_dtypes.float8_e5m2, 14)}[fmt]
    v = np.moveaxis(np.asarray(x, np.float32).astype(ml_dtypes.bfloat16).astype(np.float64), axis, -1)
    blocks = v.reshape(v.shape[:-1] + (-1, 32))
    amax = np.abs(blocks).max(-1, keepdims=True)
    byte = np.maximum(np.where(amax > 0, np.frexp(amax)[1] - 1 + 127, 0) - down, 1)
    scale = np.exp2(byte - 127.0)
    codes = (blocks / scale).astype(np.float32).astype(dtype).astype(np.float64)
    return np.moveaxis((codes * scale).reshape(v.shape), -1, axis)


WIDE = False


def mx_kscale(k):
    if not WIDE:
        return np.ones(k)
    levels = np.array([10, -10, 5, -5, 0])
    if k % 512:
        return np.exp2(np.random.permutation(np.resize(levels, k // 32))).repeat(32)
    a = np.empty((k // 512, 16))
    for p in range(k // 512):
        a[p, :8] = np.random.permutation(np.resize(levels, 8))
        for g in range(8):
            far = levels[np.abs(levels - a[p, g]) >= 10]
            a[p, g + 8] = far[np.random.randint(len(far))]
    return np.exp2(a.ravel()).repeat(32)


BF16 = ml_dtypes.bfloat16


def bf(x):
    return np.asarray(x, np.float32).astype(BF16)


def f64(x):
    return np.asarray(x).astype(np.float64)


E2M1 = np.array([0.0, 0.5, 1.0, 1.5, 2.0, 3.0, 4.0, 6.0, -0.0, -0.5, -1.0, -1.5, -2.0, -3.0, -4.0, -6.0])


def pack_weight(w, fmt):
    k, n = w.shape
    w = f64(bf(w)).reshape(k // 32, 32, n)
    amax = np.abs(w).max(1)
    if fmt == "e4m3":
        byte = np.frexp(amax)[1] - 1 + 127 - 7
    else:
        mant, ex = np.frexp(amax / 6.0)
        byte = np.where(mant > 0.5, ex, ex - 1) + 127
    byte = np.clip(np.where(amax > 0, byte, 1), 1, 254)
    scaled = (w * np.exp2(127.0 - byte)[:, None, :]).reshape(k, n).astype(np.float32)
    by_word = np.ascontiguousarray(scaled.reshape(k // 512, 128, 4, n).transpose(0, 1, 3, 2))
    if fmt == "e4m3":
        words = by_word.astype(ml_dtypes.float8_e4m3fn).view(np.uint8)
    else:
        c = by_word.astype(ml_dtypes.float4_e2m1fn).view(np.uint8) & 0xF
        words = c[..., 0::2] | (c[..., 1::2] << 4)
    return np.ascontiguousarray(words), np.ascontiguousarray(byte.astype(np.uint8).reshape(k // 512, 16, n))


def unpack_weight(words, scales, fmt):
    g, p, n, _ = words.shape
    if fmt == "e4m3":
        vals = np.ascontiguousarray(words).view(ml_dtypes.float8_e4m3fn).astype(np.float64)
    else:
        nib = np.empty((g, p, n, 4), np.uint8)
        nib[..., 0::2] = words & 0xF
        nib[..., 1::2] = words >> 4
        vals = E2M1[nib]
    vals = vals * np.repeat(np.exp2(scales.astype(np.float64) - 127.0), 8, axis=1)[..., None]
    return vals.transpose(0, 1, 3, 2).reshape(g * 512, n)
def pack4(w):
    words, scales = pack_weight(w, "e2m1")
    return words.reshape(words.shape[0], 128, -1), scales


def unpack4(words, scales):
    return unpack_weight(words.reshape(words.shape[0], 128, -1, 2), scales, "e2m1")


def planes(Y):
    n, m = Y.shape
    b = f64(bf(Y)).reshape(n // 32, 32, m)
    amax = np.abs(b).max(1)
    byte = np.clip(np.where(amax > 0, np.frexp(amax)[1] - 1 + 127 - 7, 1), 1, 254)
    codes = (b * np.exp2(127.0 - byte)[:, None, :]).reshape(n, m).astype(np.float32).astype(ml_dtypes.float8_e4m3fn).view(np.uint8)
    words = codes.reshape(n // 512, 128, 4, m).transpose(0, 1, 3, 2)
    return np.ascontiguousarray(words), np.ascontiguousarray(byte.astype(np.uint8).reshape(n // 512, 16, m))


M, N = 1280, 1024
SPREAD_MIX = 0.8
SPREAD_STRATA = 0.8
EFFECT = 0.8

def mixing():
    return 0.5 * np.exp(SPREAD_MIX * np.random.randn(N, N)) / np.sqrt(N)

def setup_inputs():
    s = mx_kscale(N)
    X = np.random.randn(N, M) * s[:, None]
    x_words, x_scales = pack_weight(X, "e4m3")
    home_words, home_scales = pack4(mixing() / s[:, None])
    work_words, work_scales = pack_weight(mixing() / s[:, None], "e4m3")
    comm = bf(mixing() / s[:, None])
    open_work = bf(0.3 + 0.7 * np.random.rand(M))
    coverage = np.random.rand(M, N)
    left = bf(np.exp(SPREAD_STRATA * np.random.randn(N))[None, :] * (1 - EFFECT * coverage))
    return {"x_words": x_words, "x_scales": x_scales,
            "home_words": home_words, "home_scales": home_scales,
            "work_words": work_words, "work_scales": work_scales,
            "comm": comm, "open_work": open_work, "left": left}

def reference(x_words, x_scales, home_words, home_scales, work_words, work_scales, comm, open_work, left):
    x = unpack_weight(x_words, x_scales, "e4m3")
    at_home = x.T @ unpack4(home_words, home_scales)
    at_work = x.T @ unpack_weight(work_words, work_scales, "e4m3")
    in_comm = x.T @ mxq(f64(comm), 0, "e4m3")
    exposure = at_home + f64(open_work)[:, None] * at_work + in_comm
    y = f64(left) * exposure
    Y = y.T
    words, scales = planes(Y)
    return y, words, scales

@@ -1,0 +1,342 @@
+from contextlib import ExitStack
+
+import concourse.mybir as mybir
+from concourse.masks import make_identity
+
+F32 = mybir.dt.float32
+BF16 = mybir.dt.bfloat16
+I32 = mybir.dt.int32
+U32 = mybir.dt.uint32
+U8 = mybir.dt.uint8
+FP8X4 = mybir.dt.float8_e4m3fn_x4
+FP4X4 = mybir.dt.float4_e2m1fn_x4
+ADD = mybir.AluOpType.add
+MULT = mybir.AluOpType.mult
+
+M, N = 1280, 1024
+FLOPS = 3 * 2 * M * N * N
+
+P = 128
+W = 512
+TILES = M // P
+UNITS = 2 * TILES
+BANKS = 8
+LEAD = 8
+X_CHUNKS = ((0, 256), (256, 768), (768, 1280))
+LEFT_CHUNKS = ((0, 0, 4), (0, 4, 10), (1, 0, 5), (1, 5, 10))
+EARLY_COLS = 768
+WORK_SHIFT = 4
+
+
+def tile_vaccinated_generation_step_k3_kernel(
+    tc, x_words, x_scales, home_words, home_scales, work_words, work_scales, comm, open_work, left,
+    out_0, out_1, out_2,
+):
+    nc = tc.nc
+    with ExitStack() as ctx:
+        keep = ctx.enter_context(tc.tile_pool(name="keep", bufs=1))
+        psum = ctx.enter_context(tc.psum_pool(name="psum", bufs=1))
+        ctx.enter_context(tc.manual_schedule())
+
+        def sb(name, shape, dtype, tag=None):
+            return keep.tile(shape, dtype, name=name, tag=tag or name, align_bytes=64)
+
+        bank_count = [0]
+
+        def new_bank():
+            n = bank_count[0]
+            bank_count[0] = n + 1
+            return psum.tile([P, W], F32, name="bank%d" % n, tag="bank%d" % (n % BANKS))
+
+        xs = sb("xs", [P, 2, M], U8)
+        ws = sb("ws", [P, 2, N], U8)
+        hs = sb("hs", [P, 2, N], U8)
+        nc.vector.memset(xs[:].bitcast(I32), 0)
+        nc.vector.memset(ws[:].bitcast(I32), 0)
+        nc.vector.memset(hs[:].bitcast(I32), 0)
+        open_rows32 = sb("open_rows32", [P, P], F32)
+        nc.vector.memset(open_rows32[:], 0.0)
+        ident = sb("ident", [P, P], F32)
+        make_identity(nc, ident[:])
+
+        def load_scales(engine, plane, scales, quadrant, shift):
+            p0 = 32 * quadrant + shift
+            engine.dma_start(
+                out=plane[p0 : p0 + 4, :, :].bitcast(I32),
+                in_=scales[:, 4 * quadrant : 4 * quadrant + 4, :].rearrange("g r n -> r g n").bitcast(I32),
+            )
+
+        xw = {}
+
+        def load_x(c):
+            c0, c1 = X_CHUNKS[c]
+            xw[c] = sb("xw%d" % c, [P, 2, c1 - c0], U32)
+            nc.sync.dma_start(
+                out=xw[c][:].bitcast(I32),
+                in_=x_words.rearrange("g p n t -> p g (n t)")[:, :, 4 * c0 : 4 * c1].bitcast(I32),
+            )
+
+        ww = {}
+
+        def load_work(h):
+            ww[h] = sb("ww%d" % h, [P, 2, W], U32)
+            nc.sync.dma_start(
+                out=ww[h][:].bitcast(I32),
+                in_=work_words.rearrange("g p n t -> p g (n t)")[:, :, 4 * W * h : 4 * W * (h + 1)].bitcast(I32),
+            )
+
+        hw = {}
+
+        def load_home(h):
+            hw[h] = sb("hw%d" % h, [P, 2, 2 * W], U8)
+            nc.sync.dma_start(
+                out=hw[h][:].bitcast(I32),
+                in_=home_words.rearrange("g p n -> p g n")[:, :, 2 * W * h : 2 * W * (h + 1)].bitcast(I32),
+            )
+
+        craw = {}
+
+        def load_comm(h, g):
+            craw[h, g] = sb("craw%d%d" % (h, g), [P, 4, W], BF16)
+            nc.sync.dma_start(
+                out=craw[h, g][:],
+                in_=comm[W * g : W * (g + 1), W * h : W * (h + 1)].rearrange("(p t) n -> p t n", t=4),
+            )
+
+        left_of = {}
+
+        def load_left(c):
+            h, t0, t1 = LEFT_CHUNKS[c]
+            rows = sb("left%d" % c, [P, t1 - t0, W], BF16)
+            nc.sync.dma_start(
+                out=rows[:],
+                in_=left[P * t0 : P * t1, W * h : W * (h + 1)].rearrange("(t p) n -> p t n", p=P),
+            )
+            for t in range(t0, t1):
+                left_of[TILES * h + t] = rows[:, t - t0, :]
+
+        for q in range(2):
+            load_scales(nc.scalar, xs, x_scales, q, 0)
+        load_x(0)
+        load_work(0)
+        for q in range(2, 4):
+            load_scales(nc.scalar, xs, x_scales, q, 0)
+        for q in range(4):
+            load_scales(nc.scalar, ws, work_scales, q, WORK_SHIFT)
+        load_x(1)
+        load_comm(0, 0)
+        load_comm(0, 1)
+        open_rows = sb("open_rows", [TILES, P], BF16)
+        nc.gpsimd.dma_start(out=open_rows[:], in_=open_work.rearrange("(t p) -> t p", p=P))
+        load_x(2)
+        for q in range(4):
+            load_scales(nc.sync, hs, home_scales, q, 0)
+        load_home(0)
+        load_comm(1, 0)
+        load_left(0)
+        load_comm(1, 1)
+        load_work(1)
+        load_left(1)
+        load_home(1)
+        load_left(2)
+        load_left(3)
+
+        def x_operand(t, g):
+            c = [k for k in range(len(X_CHUNKS)) if X_CHUNKS[k][0] <= P * t < X_CHUNKS[k][1]][0]
+            c0 = P * t - X_CHUNKS[c][0]
+            return xw[c][:, g, c0 : c0 + P].bitcast(FP8X4), xs[:, g, P * t : P * (t + 1)]
+
+        cgrp, ccodes, cscales = {}, {}, {}
+
+        def interleave_comm(h, g, part, parts):
+            if part == 0:
+                cgrp[h, g] = sb("cgrp%d%d" % (h, g), [P, W, 4], BF16)
+            cols = slice(part * W // parts, (part + 1) * W // parts)
+            nc.vector.tensor_copy(
+                out=cgrp[h, g][:, cols, :].rearrange("p (c i) t -> p c t i", i=4),
+                in_=craw[h, g][:, :, cols].rearrange("p t (c i) -> p c t i", i=4),
+            )
+
+        def quantize_comm(h, g):
+            ccodes[h, g] = sb("ccodes%d%d" % (h, g), [P, W], U32)
+            cscales[h, g] = sb("cscales%d%d" % (h, g), [P, W], U8)
+            nc.vector.quantize_mx(
+                out=ccodes[h, g][:].bitcast(FP8X4),
+                scales=cscales[h, g][:],
+                in_=cgrp[h, g][:].rearrange("p n t -> p (n t)"),
+            )
+
+        work_bank, work_sb, sum_bank = {}, {}, {}
+
+        def work_passes(j):
+            h, t = divmod(j, TILES)
+            work_bank[j] = new_bank()
+            for g in range(2):
+                codes, scales = x_operand(t, g)
+                nc.tensor.matmul_mx(
+                    out=work_bank[j][:], lhsT=codes, lhsT_scale=scales,
+                    rhs=ww[h][:, g, :].bitcast(FP8X4), rhs_scale=ws[WORK_SHIFT:, g, W * h : W * (h + 1)],
+                    start=(g == 0), stop=(g == 1),
+                )
+
+        def work_copy(j):
+            work_sb[j] = sb("work%d" % j, [P, W], F32, tag="work%d" % (j % 12))
+            nc.scalar.copy(out=work_sb[j][:], in_=work_bank[j][:])
+
+        def sum_passes(j):
+            h, t = divmod(j, TILES)
+            sum_bank[j] = new_bank()
+            for g in range(2):
+                codes, scales = x_operand(t, g)
+                nc.tensor.matmul_mx(
+                    out=sum_bank[j][:], lhsT=codes, lhsT_scale=scales,
+                    rhs=hw[h][:, g, :].bitcast(FP4X4), rhs_scale=hs[:, g, W * h : W * (h + 1)],
+                    start=(g == 0), stop=False,
+                )
+            for g in range(2):
+                codes, scales = x_operand(t, g)
+                nc.tensor.matmul_mx(
+                    out=sum_bank[j][:], lhsT=codes, lhsT_scale=scales,
+                    rhs=ccodes[h, g][:].bitcast(FP8X4), rhs_scale=cscales[h, g][:],
+                    start=False, stop=(g == 1),
+                )
+
+        open_cols = sb("open_cols", [P, TILES], F32)
+        exposure, y, ybf = {}, {}, {}
+        halves = (slice(0, W // 2), slice(W // 2, W))
+
+        def add_up(j):
+            t = j % TILES
+            exposure[j] = sb("exposure%d" % j, [P, W], F32, tag="exposure%d" % (j % 3))
+            for cols in halves:
+                nc.vector.scalar_tensor_tensor(
+                    out=exposure[j][:, cols], in0=work_sb[j][:, cols], scalar=open_cols[:, t : t + 1],
+                    in1=sum_bank[j][:, cols], op0=MULT, op1=ADD,
+                )
+
+        def times_left(j, pieces):
+            h, t = divmod(j, TILES)
+            y[j] = sb("y%d" % j, [P, W], F32, tag="y%d" % (j % 10))
+            for cols in pieces:
+                nc.vector.tensor_tensor(
+                    out=y[j][:, cols], in0=exposure[j][:, cols], in1=left_of[j][:, cols], op=MULT
+                )
+            nc.sync.dma_start(out=out_0[P * t : P * (t + 1), W * h : W * (h + 1)], in_=y[j][:])
+
+        def new_ybf(j):
+            ybf[j] = sb("ybf%d" % j, [P, W], BF16, tag="ybf%d" % (j % 8))
+            return ybf[j][:].rearrange("b (u p e) -> b u p e", u=2, e=2)
+
+        def round_y(j):
+            nc.scalar.copy(out=new_ybf(j), in_=y[j][:].rearrange("b (p u e) -> b u p e", u=2, e=2))
+
+        def times_left_rounded(j):
+            sorted_out = new_ybf(j)
+            for k in range(2):
+                nc.vector.tensor_tensor(
+                    out=sorted_out[:, :, 64 * k : 64 * (k + 1), :],
+                    in0=exposure[j][:, halves[k]].rearrange("b (p u e) -> b u p e", u=2, e=2),
+                    in1=left_of[j][:, halves[k]].rearrange("b (p u e) -> b u p e", u=2, e=2),
+                    op=MULT,
+                )
+
+        turn_bank, turned = {}, {}
+
+        def turn(j, count):
+            turn_bank[j] = new_bank()
+            view = turn_bank[j][:, : 2 * P * count].rearrange("p (u m) -> p u m", u=2)
+            for k in range(count):
+                words = ybf[j + k][:].bitcast(F32)
+                for u in range(2):
+                    nc.tensor.transpose(view[:, u, P * k : P * (k + 1)], words[:, P * u : P * (u + 1)], ident[:])
+
+        def turn_copy(j, count):
+            turned[j] = sb("turned%d" % j, [P, 4 * P * count], BF16, tag="turned%d" % ((j // 2 + j % 2) % 3))
+            nc.scalar.copy(
+                out=turned[j][:].bitcast(F32).rearrange("p (m u) -> p m u", u=2),
+                in_=turn_bank[j][:, : 2 * P * count].rearrange("p (u m) -> p m u", u=2),
+            )
+
+        early_scales = sb("early_scales", [P, 2, EARLY_COLS], U8)
+        late_scales = sb("late_scales", [P, 2, M - EARLY_COLS], U8)
+
+        def quantize_y(j, count):
+            h, t = divmod(j, TILES)
+            c0, c1 = P * t, P * (t + count)
+            codes = sb("codes%d" % j, [P, c1 - c0], U32, tag="codes%d" % ((j // 2 + j % 2) % 4))
+            if c0 < EARLY_COLS:
+                scales = early_scales[:, h, c0:c1]
+            else:
+                scales = late_scales[:, h, c0 - EARLY_COLS : c1 - EARLY_COLS]
+            nc.vector.quantize_mx(out=codes[:].bitcast(FP8X4), scales=scales, in_=turned[j][:])
+            nc.sync.dma_start(
+                out=out_1[h].rearrange("p m t -> p (m t)")[:, 4 * c0 : 4 * c1].bitcast(I32),
+                in_=codes[:].bitcast(I32),
+            )
+
+        def store_scales(engine, plane, c0, c1, quadrant):
+            engine.dma_start(
+                out=out_2[:, 4 * quadrant : 4 * quadrant + 4, c0:c1].rearrange("g r m -> r g m").bitcast(I32),
+                in_=plane[32 * quadrant : 32 * quadrant + 4, :, :].bitcast(I32),
+            )
+
+        for j in range(LEAD):
+            work_passes(j)
+            work_copy(j)
+        nc.vector.tensor_copy(out=open_rows32[:TILES, :], in_=open_rows[:])
+        interleave_comm(0, 0, 0, 1)
+        interleave_comm(0, 1, 0, 1)
+        quantize_comm(0, 0)
+        quantize_comm(0, 1)
+        open_bank = new_bank()
+        nc.tensor.transpose(open_bank[:, :P], open_rows32[:], ident[:])
+        nc.scalar.copy(out=open_cols[:], in_=open_bank[:, :TILES])
+        interleave_comm(1, 0, 0, 1)
+
+        work_steps = [s for s in range(UNITS - 1) if s < 6 or s % 2 == 1]
+        turn_steps = (5, 9, 13, 17)
+        for s in range(UNITS):
+            ahead = LEAD + work_steps.index(s) if s in work_steps else None
+            if ahead is not None:
+                work_passes(ahead)
+            sum_passes(s)
+            if s - 1 in turn_steps:
+                turn_copy(s - 6, 2)
+                turn_copy(s - 4, 2)
+            if ahead is not None:
+                work_copy(ahead)
+            if s >= 1:
+                add_up(s - 1)
+                times_left(s - 1, halves)
+                round_y(s - 1)
+            if s == 1:
+                quantize_comm(1, 0)
+            if 2 <= s <= 5:
+                interleave_comm(1, 1, s - 2, 4)
+            if s == 7:
+                quantize_comm(1, 1)
+            if s - 1 in turn_steps:
+                quantize_y(s - 6, 2)
+                quantize_y(s - 4, 2)
+            if s - 1 == turn_steps[-1]:
+                for q in range(4):
+                    store_scales(nc.sync, early_scales, 0, EARLY_COLS, q)
+            if s in turn_steps:
+                turn(s - 5, 2)
+                turn(s - 3, 2)
+
+        last = UNITS - 1
+        turn(last - 3, 2)
+        turn(last - 1, 1)
+        turn_copy(last - 3, 2)
+        turn_copy(last - 1, 1)
+        add_up(last)
+        times_left_rounded(last)
+        turn(last, 1)
+        turn_copy(last, 1)
+        times_left(last, (slice(0, W),))
+        quantize_y(last - 3, 2)
+        quantize_y(last - 1, 1)
+        quantize_y(last, 1)
+        for q in range(4):
+            store_scales(nc.sync if q < 2 else nc.scalar, late_scales, EARLY_COLS, M, q)

@@ -21,9 +21,9 @@ W = 512
 TILES = M // P
 UNITS = 2 * TILES
 BANKS = 8
-LEAD = 8
+LEAD = 10
 X_CHUNKS = ((0, 256), (256, 768), (768, 1280))
-LEFT_CHUNKS = ((0, 0, 4), (0, 4, 10), (1, 0, 5), (1, 5, 10))
+LEFT_CHUNKS = ((0, 0, 2), (0, 2, 6), (0, 6, 10), (1, 0, 5), (1, 5, 10))
 EARLY_COLS = 768
 WORK_SHIFT = 4
 
@@ -119,10 +119,12 @@ def tile_vaccinated_generation_step_k3_kernel(
             load_scales(nc.scalar, xs, x_scales, q, 0)
         load_x(0)
         load_work(0)
+        for q in range(2):
+            load_scales(nc.sync, ws, work_scales, q, WORK_SHIFT)
         for q in range(2, 4):
             load_scales(nc.scalar, xs, x_scales, q, 0)
-        for q in range(4):
-            load_scales(nc.scalar, ws, work_scales, q, WORK_SHIFT)
+        load_scales(nc.sync, ws, work_scales, 2, WORK_SHIFT)
+        load_scales(nc.scalar, ws, work_scales, 3, WORK_SHIFT)
         load_x(1)
         load_comm(0, 0)
         load_comm(0, 1)
@@ -134,12 +136,13 @@ def tile_vaccinated_generation_step_k3_kernel(
         load_home(0)
         load_comm(1, 0)
         load_left(0)
-        load_comm(1, 1)
         load_work(1)
         load_left(1)
-        load_home(1)
+        load_comm(1, 1)
         load_left(2)
+        load_home(1)
         load_left(3)
+        load_left(4)
 
         def x_operand(t, g):
             c = [k for k in range(len(X_CHUNKS)) if X_CHUNKS[k][0] <= P * t < X_CHUNKS[k][1]][0]
@@ -153,8 +156,8 @@ def tile_vaccinated_generation_step_k3_kernel(
                 cgrp[h, g] = sb("cgrp%d%d" % (h, g), [P, W, 4], BF16)
             cols = slice(part * W // parts, (part + 1) * W // parts)
             nc.vector.tensor_copy(
-                out=cgrp[h, g][:, cols, :].rearrange("p (c i) t -> p c t i", i=4),
-                in_=craw[h, g][:, :, cols].rearrange("p t (c i) -> p c t i", i=4),
+                out=cgrp[h, g][:, cols, :],
+                in_=craw[h, g][:, :, cols].rearrange("p t n -> p n t"),
             )
 
         def quantize_comm(h, g):
@@ -293,16 +296,15 @@ def tile_vaccinated_generation_step_k3_kernel(
         nc.scalar.copy(out=open_cols[:], in_=open_bank[:, :TILES])
         interleave_comm(1, 0, 0, 1)
 
-        work_steps = [s for s in range(UNITS - 1) if s < 6 or s % 2 == 1]
-        turn_steps = (5, 9, 13, 17)
+        work_steps = [s for s in range(2, UNITS - 1) if s < 6 or s % 2 == 1]
+        turn_runs = {7: (0, 2, 4), 13: (6, 8, 10), 17: (12, 14)}
         for s in range(UNITS):
             ahead = LEAD + work_steps.index(s) if s in work_steps else None
             if ahead is not None:
                 work_passes(ahead)
             sum_passes(s)
-            if s - 1 in turn_steps:
-                turn_copy(s - 6, 2)
-                turn_copy(s - 4, 2)
+            for j in turn_runs.get(s - 1, ()):
+                turn_copy(j, 2)
             if ahead is not None:
                 work_copy(ahead)
             if s >= 1:
@@ -311,19 +313,17 @@ def tile_vaccinated_generation_step_k3_kernel(
                 round_y(s - 1)
             if s == 1:
                 quantize_comm(1, 0)
-            if 2 <= s <= 5:
-                interleave_comm(1, 1, s - 2, 4)
+            if 3 <= s <= 6:
+                interleave_comm(1, 1, s - 3, 4)
             if s == 7:
                 quantize_comm(1, 1)
-            if s - 1 in turn_steps:
-                quantize_y(s - 6, 2)
-                quantize_y(s - 4, 2)
-            if s - 1 == turn_steps[-1]:
+            for j in turn_runs.get(s - 1, ()):
+                quantize_y(j, 2)
+            if s - 1 == 17:
                 for q in range(4):
                     store_scales(nc.sync, early_scales, 0, EARLY_COLS, q)
-            if s in turn_steps:
-                turn(s - 5, 2)
-                turn(s - 3, 2)
+            for j in turn_runs.get(s, ()):
+                turn(j, 2)
 
         last = UNITS - 1
         turn(last - 3, 2)

@@ -21,8 +21,9 @@ W = 512
 TILES = M // P
 UNITS = 2 * TILES
 BANKS = 8
-LEAD = 10
-X_CHUNKS = ((0, 256), (256, 768), (768, 1280))
+HEAD = 4
+VECTOR_COLS = 352
+X_CHUNKS = ((0, 256), (256, 512), (512, 896), (896, 1280))
 LEFT_CHUNKS = ((0, 0, 2), (0, 2, 6), (0, 6, 10), (1, 0, 5), (1, 5, 10))
 EARLY_COLS = 768
 WORK_SHIFT = 4
@@ -52,12 +53,15 @@ def tile_vaccinated_generation_step_k3_kernel(
         ws = sb("ws", [P, 2, N], U8)
         hs = sb("hs", [P, 2, N], U8)
         nc.vector.memset(xs[:].bitcast(I32), 0)
-        nc.vector.memset(ws[:].bitcast(I32), 0)
         nc.vector.memset(hs[:].bitcast(I32), 0)
+        nc.vector.memset(ws[:].bitcast(I32), 0)
+        open_rows = sb("open_rows", [TILES, P], BF16)
+        nc.gpsimd.dma_start(out=open_rows[:], in_=open_work.rearrange("(t p) -> t p", p=P))
         open_rows32 = sb("open_rows32", [P, P], F32)
-        nc.vector.memset(open_rows32[:], 0.0)
+        nc.gpsimd.memset(open_rows32[:], 0.0)
         ident = sb("ident", [P, P], F32)
         make_identity(nc, ident[:])
+        nc.gpsimd.tensor_copy(out=open_rows32[:TILES, :], in_=open_rows[:])
 
         def load_scales(engine, plane, scales, quadrant, shift):
             p0 = 32 * quadrant + shift
@@ -115,31 +119,30 @@ def tile_vaccinated_generation_step_k3_kernel(
             for t in range(t0, t1):
                 left_of[TILES * h + t] = rows[:, t - t0, :]
 
+        load_comm(0, 0)
         for q in range(2):
             load_scales(nc.scalar, xs, x_scales, q, 0)
         load_x(0)
-        load_work(0)
-        for q in range(2):
-            load_scales(nc.sync, ws, work_scales, q, WORK_SHIFT)
         for q in range(2, 4):
-            load_scales(nc.scalar, xs, x_scales, q, 0)
-        load_scales(nc.sync, ws, work_scales, 2, WORK_SHIFT)
-        load_scales(nc.scalar, ws, work_scales, 3, WORK_SHIFT)
-        load_x(1)
-        load_comm(0, 0)
+            load_scales(nc.sync, xs, x_scales, q, 0)
         load_comm(0, 1)
-        open_rows = sb("open_rows", [TILES, P], BF16)
-        nc.gpsimd.dma_start(out=open_rows[:], in_=open_work.rearrange("(t p) -> t p", p=P))
-        load_x(2)
-        for q in range(4):
-            load_scales(nc.sync, hs, home_scales, q, 0)
+        load_x(1)
         load_home(0)
-        load_comm(1, 0)
+        for q in range(2):
+            load_scales(nc.sync, hs, home_scales, q, 0)
+        load_work(0)
+        for q in range(2, 4):
+            load_scales(nc.sync, hs, home_scales, q, 0)
+        for q in range(4):
+            load_scales(nc.sync, ws, work_scales, q, WORK_SHIFT)
         load_left(0)
-        load_work(1)
+        load_x(2)
         load_left(1)
+        load_comm(1, 0)
+        load_x(3)
         load_comm(1, 1)
         load_left(2)
+        load_work(1)
         load_home(1)
         load_left(3)
         load_left(4)
@@ -151,14 +154,11 @@ def tile_vaccinated_generation_step_k3_kernel(
 
         cgrp, ccodes, cscales = {}, {}, {}
 
-        def interleave_comm(h, g, part, parts):
-            if part == 0:
-                cgrp[h, g] = sb("cgrp%d%d" % (h, g), [P, W, 4], BF16)
-            cols = slice(part * W // parts, (part + 1) * W // parts)
-            nc.vector.tensor_copy(
-                out=cgrp[h, g][:, cols, :],
-                in_=craw[h, g][:, :, cols].rearrange("p t n -> p n t"),
-            )
+        def interleave_comm(h, g):
+            cgrp[h, g] = sb("cgrp%d%d" % (h, g), [P, W, 4], BF16)
+            by_column = craw[h, g][:].rearrange("p t n -> p n t")
+            nc.vector.tensor_copy(out=cgrp[h, g][:, :VECTOR_COLS, :], in_=by_column[:, :VECTOR_COLS, :])
+            nc.scalar.copy(out=cgrp[h, g][:, VECTOR_COLS:, :], in_=by_column[:, VECTOR_COLS:, :])
 
         def quantize_comm(h, g):
             ccodes[h, g] = sb("ccodes%d%d" % (h, g), [P, W], U32)
@@ -183,24 +183,27 @@ def tile_vaccinated_generation_step_k3_kernel(
                 )
 
         def work_copy(j):
-            work_sb[j] = sb("work%d" % j, [P, W], F32, tag="work%d" % (j % 12))
+            work_sb[j] = sb("work%d" % j, [P, W], F32, tag="work%d" % (j % 4))
             nc.scalar.copy(out=work_sb[j][:], in_=work_bank[j][:])
 
-        def sum_passes(j):
+        def comm_pass(j, g):
             h, t = divmod(j, TILES)
-            sum_bank[j] = new_bank()
+            if g == 0:
+                sum_bank[j] = new_bank()
+            codes, scales = x_operand(t, g)
+            nc.tensor.matmul_mx(
+                out=sum_bank[j][:], lhsT=codes, lhsT_scale=scales,
+                rhs=ccodes[h, g][:].bitcast(FP8X4), rhs_scale=cscales[h, g][:],
+                start=(g == 0), stop=False,
+            )
+
+        def home_passes(j):
+            h, t = divmod(j, TILES)
             for g in range(2):
                 codes, scales = x_operand(t, g)
                 nc.tensor.matmul_mx(
                     out=sum_bank[j][:], lhsT=codes, lhsT_scale=scales,
                     rhs=hw[h][:, g, :].bitcast(FP4X4), rhs_scale=hs[:, g, W * h : W * (h + 1)],
-                    start=(g == 0), stop=False,
-                )
-            for g in range(2):
-                codes, scales = x_operand(t, g)
-                nc.tensor.matmul_mx(
-                    out=sum_bank[j][:], lhsT=codes, lhsT_scale=scales,
-                    rhs=ccodes[h, g][:].bitcast(FP8X4), rhs_scale=cscales[h, g][:],
                     start=False, stop=(g == 1),
                 )
 
@@ -219,7 +222,7 @@ def tile_vaccinated_generation_step_k3_kernel(
 
         def times_left(j, pieces):
             h, t = divmod(j, TILES)
-            y[j] = sb("y%d" % j, [P, W], F32, tag="y%d" % (j % 10))
+            y[j] = sb("y%d" % j, [P, W], F32, tag="y%d" % (j % 12))
             for cols in pieces:
                 nc.vector.tensor_tensor(
                     out=y[j][:, cols], in0=exposure[j][:, cols], in1=left_of[j][:, cols], op=MULT
@@ -263,19 +266,28 @@ def tile_vaccinated_generation_step_k3_kernel(
         early_scales = sb("early_scales", [P, 2, EARLY_COLS], U8)
         late_scales = sb("late_scales", [P, 2, M - EARLY_COLS], U8)
 
+        pair_codes = {}
+
         def quantize_y(j, count):
             h, t = divmod(j, TILES)
+            pair = j // 2
+            if j % 2 == 0:
+                pair_codes[pair] = sb("codes%d" % pair, [P, 2 * P], U32, tag="codes%d" % (pair % 4))
+            codes = pair_codes[pair]
             c0, c1 = P * t, P * (t + count)
-            codes = sb("codes%d" % j, [P, c1 - c0], U32, tag="codes%d" % ((j // 2 + j % 2) % 4))
             if c0 < EARLY_COLS:
                 scales = early_scales[:, h, c0:c1]
             else:
                 scales = late_scales[:, h, c0 - EARLY_COLS : c1 - EARLY_COLS]
-            nc.vector.quantize_mx(out=codes[:].bitcast(FP8X4), scales=scales, in_=turned[j][:])
-            nc.sync.dma_start(
-                out=out_1[h].rearrange("p m t -> p (m t)")[:, 4 * c0 : 4 * c1].bitcast(I32),
-                in_=codes[:].bitcast(I32),
+            w0 = P * (j % 2)
+            nc.vector.quantize_mx(
+                out=codes[:, w0 : w0 + P * count].bitcast(FP8X4), scales=scales, in_=turned[j][:]
             )
+            if (j + count) % 2 == 0:
+                nc.sync.dma_start(
+                    out=out_1[h].rearrange("p m t -> p (m t)")[:, 4 * (c1 - 2 * P) : 4 * c1].bitcast(I32),
+                    in_=codes[:].bitcast(I32),
+                )
 
         def store_scales(engine, plane, c0, c1, quadrant):
             engine.dma_start(
@@ -283,40 +295,35 @@ def tile_vaccinated_generation_step_k3_kernel(
                 in_=plane[32 * quadrant : 32 * quadrant + 4, :, :].bitcast(I32),
             )
 
-        for j in range(LEAD):
-            work_passes(j)
-            work_copy(j)
-        nc.vector.tensor_copy(out=open_rows32[:TILES, :], in_=open_rows[:])
-        interleave_comm(0, 0, 0, 1)
-        interleave_comm(0, 1, 0, 1)
-        quantize_comm(0, 0)
-        quantize_comm(0, 1)
+        for g in range(2):
+            interleave_comm(0, g)
+            quantize_comm(0, g)
+        for j in range(HEAD):
+            comm_pass(j, 0)
         open_bank = new_bank()
         nc.tensor.transpose(open_bank[:, :P], open_rows32[:], ident[:])
         nc.scalar.copy(out=open_cols[:], in_=open_bank[:, :TILES])
-        interleave_comm(1, 0, 0, 1)
+        for j in range(HEAD):
+            comm_pass(j, 1)
 
-        work_steps = [s for s in range(2, UNITS - 1) if s < 6 or s % 2 == 1]
         turn_runs = {7: (0, 2, 4), 13: (6, 8, 10), 17: (12, 14)}
         for s in range(UNITS):
-            ahead = LEAD + work_steps.index(s) if s in work_steps else None
-            if ahead is not None:
-                work_passes(ahead)
-            sum_passes(s)
+            work_passes(s)
+            if s >= HEAD:
+                comm_pass(s, 0)
+                comm_pass(s, 1)
+            home_passes(s)
             for j in turn_runs.get(s - 1, ()):
                 turn_copy(j, 2)
-            if ahead is not None:
-                work_copy(ahead)
+            work_copy(s)
             if s >= 1:
                 add_up(s - 1)
                 times_left(s - 1, halves)
                 round_y(s - 1)
-            if s == 1:
-                quantize_comm(1, 0)
-            if 3 <= s <= 6:
-                interleave_comm(1, 1, s - 3, 4)
-            if s == 7:
-                quantize_comm(1, 1)
+            if s in (4, 6):
+                interleave_comm(1, (s - 4) // 2)
+            if s in (5, 7):
+                quantize_comm(1, (s - 5) // 2)
             for j in turn_runs.get(s - 1, ()):
                 quantize_y(j, 2)
             if s - 1 == 17:

@@ -20,13 +20,26 @@ P = 128
 W = 512
 TILES = M // P
 UNITS = 2 * TILES
-BANKS = 8
-HEAD = 4
+LAST = UNITS - 1
+
+SUM_BANKS = 4
+SHORT_BANKS = 4
+HEAD_UNITS = SUM_BANKS
+HEAD_HOME_UNITS = 2
+
 VECTOR_COLS = 352
-X_CHUNKS = ((0, 256), (256, 512), (512, 896), (896, 1280))
-LEFT_CHUNKS = ((0, 0, 2), (0, 2, 6), (0, 6, 10), (1, 0, 5), (1, 5, 10))
-EARLY_COLS = 768
+SECOND_HALF_STEPS = (5, 7)
+
+X_LOADS = ((0, 256), (256, 512), (512, 896), (896, 1280))
+LEFT_LOADS = ((0, 0, 2), (0, 2, 6), (0, 6, 10), (1, 0, 5), (1, 5, 10))
 WORK_SHIFT = 4
+
+TURN_RUNS = {8: (0, 2, 4), 14: (6, 8, 10), 17: (12, 14)}
+CATCH_UP_STEP = 16
+CODE_STORES = ((0, 6), (6, 10), (10, 12), (12, 16), (16, 18), (18, 20))
+EARLY_COLS = 768
+
+WORK_TILES, EXPOSURE_TILES, ROUNDED_TILES, TURNED_TILES = 6, 3, 8, 3
 
 
 def tile_vaccinated_generation_step_k3_kernel(
@@ -42,26 +55,27 @@ def tile_vaccinated_generation_step_k3_kernel(
         def sb(name, shape, dtype, tag=None):
             return keep.tile(shape, dtype, name=name, tag=tag or name, align_bytes=64)
 
-        bank_count = [0]
+        banks_taken = {"sum": 0, "short": 0}
 
-        def new_bank():
-            n = bank_count[0]
-            bank_count[0] = n + 1
-            return psum.tile([P, W], F32, name="bank%d" % n, tag="bank%d" % (n % BANKS))
+        def new_bank(kind, count):
+            n = banks_taken[kind]
+            banks_taken[kind] = n + 1
+            return psum.tile([P, W], F32, name="%s%d" % (kind, n), tag="%s%d" % (kind, n % count))
 
-        xs = sb("xs", [P, 2, M], U8)
-        ws = sb("ws", [P, 2, N], U8)
-        hs = sb("hs", [P, 2, N], U8)
-        nc.vector.memset(xs[:].bitcast(I32), 0)
-        nc.vector.memset(hs[:].bitcast(I32), 0)
-        nc.vector.memset(ws[:].bitcast(I32), 0)
+        x_plane = sb("x_plane", [P, 2, M], U8)
+        work_plane = sb("work_plane", [P, 2, N], U8)
+        home_plane = sb("home_plane", [P, 2, N], U8)
+        nc.vector.memset(x_plane[:].bitcast(I32), 0)
+        nc.vector.memset(home_plane[:].bitcast(I32), 0)
+        nc.vector.memset(work_plane[:].bitcast(I32), 0)
+
         open_rows = sb("open_rows", [TILES, P], BF16)
         nc.gpsimd.dma_start(out=open_rows[:], in_=open_work.rearrange("(t p) -> t p", p=P))
-        open_rows32 = sb("open_rows32", [P, P], F32)
-        nc.gpsimd.memset(open_rows32[:], 0.0)
+        open_square = sb("open_square", [P, P], F32)
+        nc.gpsimd.memset(open_square[:], 0.0)
         ident = sb("ident", [P, P], F32)
         make_identity(nc, ident[:])
-        nc.gpsimd.tensor_copy(out=open_rows32[:TILES, :], in_=open_rows[:])
+        nc.gpsimd.tensor_copy(out=open_square[:TILES, :], in_=open_rows[:])
 
         def load_scales(engine, plane, scales, quadrant, shift):
             p0 = 32 * quadrant + shift
@@ -70,47 +84,39 @@ def tile_vaccinated_generation_step_k3_kernel(
                 in_=scales[:, 4 * quadrant : 4 * quadrant + 4, :].rearrange("g r n -> r g n").bitcast(I32),
             )
 
-        xw = {}
+        x_codes, work_codes, home_codes, comm_rows, left_of = {}, {}, {}, {}, {}
 
         def load_x(c):
-            c0, c1 = X_CHUNKS[c]
-            xw[c] = sb("xw%d" % c, [P, 2, c1 - c0], U32)
+            c0, c1 = X_LOADS[c]
+            x_codes[c] = sb("x_codes%d" % c, [P, 2, c1 - c0], U32)
             nc.sync.dma_start(
-                out=xw[c][:].bitcast(I32),
+                out=x_codes[c][:].bitcast(I32),
                 in_=x_words.rearrange("g p n t -> p g (n t)")[:, :, 4 * c0 : 4 * c1].bitcast(I32),
             )
 
-        ww = {}
-
         def load_work(h):
-            ww[h] = sb("ww%d" % h, [P, 2, W], U32)
+            work_codes[h] = sb("work_codes%d" % h, [P, 2, W], U32)
             nc.sync.dma_start(
-                out=ww[h][:].bitcast(I32),
+                out=work_codes[h][:].bitcast(I32),
                 in_=work_words.rearrange("g p n t -> p g (n t)")[:, :, 4 * W * h : 4 * W * (h + 1)].bitcast(I32),
             )
 
-        hw = {}
-
         def load_home(h):
-            hw[h] = sb("hw%d" % h, [P, 2, 2 * W], U8)
+            home_codes[h] = sb("home_codes%d" % h, [P, 2, 2 * W], U8)
             nc.sync.dma_start(
-                out=hw[h][:].bitcast(I32),
+                out=home_codes[h][:].bitcast(I32),
                 in_=home_words.rearrange("g p n -> p g n")[:, :, 2 * W * h : 2 * W * (h + 1)].bitcast(I32),
             )
 
-        craw = {}
-
         def load_comm(h, g):
-            craw[h, g] = sb("craw%d%d" % (h, g), [P, 4, W], BF16)
+            comm_rows[h, g] = sb("comm_rows%d%d" % (h, g), [P, 4, W], BF16)
             nc.sync.dma_start(
-                out=craw[h, g][:],
+                out=comm_rows[h, g][:],
                 in_=comm[W * g : W * (g + 1), W * h : W * (h + 1)].rearrange("(p t) n -> p t n", t=4),
             )
 
-        left_of = {}
-
         def load_left(c):
-            h, t0, t1 = LEFT_CHUNKS[c]
+            h, t0, t1 = LEFT_LOADS[c]
             rows = sb("left%d" % c, [P, t1 - t0, W], BF16)
             nc.sync.dma_start(
                 out=rows[:],
@@ -121,20 +127,18 @@ def tile_vaccinated_generation_step_k3_kernel(
 
         load_comm(0, 0)
         for q in range(2):
-            load_scales(nc.scalar, xs, x_scales, q, 0)
+            load_scales(nc.scalar, x_plane, x_scales, q, 0)
         load_x(0)
         for q in range(2, 4):
-            load_scales(nc.sync, xs, x_scales, q, 0)
+            load_scales(nc.sync, x_plane, x_scales, q, 0)
         load_comm(0, 1)
         load_x(1)
         load_home(0)
-        for q in range(2):
-            load_scales(nc.sync, hs, home_scales, q, 0)
-        load_work(0)
-        for q in range(2, 4):
-            load_scales(nc.sync, hs, home_scales, q, 0)
         for q in range(4):
-            load_scales(nc.sync, ws, work_scales, q, WORK_SHIFT)
+            load_scales(nc.sync, home_plane, home_scales, q, 0)
+        load_work(0)
+        for q in range(4):
+            load_scales(nc.sync, work_plane, work_scales, q, WORK_SHIFT)
         load_left(0)
         load_x(2)
         load_left(1)
@@ -147,146 +151,143 @@ def tile_vaccinated_generation_step_k3_kernel(
         load_left(3)
         load_left(4)
 
-        def x_operand(t, g):
-            c = [k for k in range(len(X_CHUNKS)) if X_CHUNKS[k][0] <= P * t < X_CHUNKS[k][1]][0]
-            c0 = P * t - X_CHUNKS[c][0]
-            return xw[c][:, g, c0 : c0 + P].bitcast(FP8X4), xs[:, g, P * t : P * (t + 1)]
-
-        cgrp, ccodes, cscales = {}, {}, {}
+        comm_grouped, comm_codes, comm_plane = {}, {}, {}
 
         def interleave_comm(h, g):
-            cgrp[h, g] = sb("cgrp%d%d" % (h, g), [P, W, 4], BF16)
-            by_column = craw[h, g][:].rearrange("p t n -> p n t")
-            nc.vector.tensor_copy(out=cgrp[h, g][:, :VECTOR_COLS, :], in_=by_column[:, :VECTOR_COLS, :])
-            nc.scalar.copy(out=cgrp[h, g][:, VECTOR_COLS:, :], in_=by_column[:, VECTOR_COLS:, :])
+            comm_grouped[h, g] = sb("comm_grouped%d%d" % (h, g), [P, W, 4], BF16)
+            by_column = comm_rows[h, g][:].rearrange("p t n -> p n t")
+            nc.vector.tensor_copy(out=comm_grouped[h, g][:, :VECTOR_COLS, :], in_=by_column[:, :VECTOR_COLS, :])
+            nc.scalar.copy(out=comm_grouped[h, g][:, VECTOR_COLS:, :], in_=by_column[:, VECTOR_COLS:, :])
 
         def quantize_comm(h, g):
-            ccodes[h, g] = sb("ccodes%d%d" % (h, g), [P, W], U32)
-            cscales[h, g] = sb("cscales%d%d" % (h, g), [P, W], U8)
+            comm_codes[h, g] = sb("comm_codes%d%d" % (h, g), [P, W], U32)
+            comm_plane[h, g] = sb("comm_plane%d%d" % (h, g), [P, W], U8)
             nc.vector.quantize_mx(
-                out=ccodes[h, g][:].bitcast(FP8X4),
-                scales=cscales[h, g][:],
-                in_=cgrp[h, g][:].rearrange("p n t -> p (n t)"),
+                out=comm_codes[h, g][:].bitcast(FP8X4),
+                scales=comm_plane[h, g][:],
+                in_=comm_grouped[h, g][:].rearrange("p n t -> p (n t)"),
             )
 
-        work_bank, work_sb, sum_bank = {}, {}, {}
+        work_bank, work_out, sum_bank = {}, {}, {}
+
+        def mx_pass(bank, t, g, codes, plane, start, stop):
+            c = [k for k, (c0, c1) in enumerate(X_LOADS) if c0 <= P * t < c1][0]
+            w0 = P * t - X_LOADS[c][0]
+            nc.tensor.matmul_mx(
+                out=bank[:],
+                lhsT=x_codes[c][:, g, w0 : w0 + P].bitcast(FP8X4),
+                lhsT_scale=x_plane[:, g, P * t : P * (t + 1)],
+                rhs=codes,
+                rhs_scale=plane,
+                start=start,
+                stop=stop,
+            )
 
         def work_passes(j):
             h, t = divmod(j, TILES)
-            work_bank[j] = new_bank()
+            work_bank[j] = new_bank("short", SHORT_BANKS)
             for g in range(2):
-                codes, scales = x_operand(t, g)
-                nc.tensor.matmul_mx(
-                    out=work_bank[j][:], lhsT=codes, lhsT_scale=scales,
-                    rhs=ww[h][:, g, :].bitcast(FP8X4), rhs_scale=ws[WORK_SHIFT:, g, W * h : W * (h + 1)],
-                    start=(g == 0), stop=(g == 1),
+                mx_pass(
+                    work_bank[j], t, g, work_codes[h][:, g, :].bitcast(FP8X4),
+                    work_plane[WORK_SHIFT:, g, W * h : W * (h + 1)], g == 0, g == 1,
                 )
 
         def work_copy(j):
-            work_sb[j] = sb("work%d" % j, [P, W], F32, tag="work%d" % (j % 4))
-            nc.scalar.copy(out=work_sb[j][:], in_=work_bank[j][:])
+            work_out[j] = sb("work_out%d" % j, [P, W], F32, tag="work_out%d" % (j % WORK_TILES))
+            nc.scalar.copy(out=work_out[j][:], in_=work_bank[j][:])
 
         def comm_pass(j, g):
             h, t = divmod(j, TILES)
             if g == 0:
-                sum_bank[j] = new_bank()
-            codes, scales = x_operand(t, g)
-            nc.tensor.matmul_mx(
-                out=sum_bank[j][:], lhsT=codes, lhsT_scale=scales,
-                rhs=ccodes[h, g][:].bitcast(FP8X4), rhs_scale=cscales[h, g][:],
-                start=(g == 0), stop=False,
-            )
+                sum_bank[j] = new_bank("sum", SUM_BANKS)
+            mx_pass(sum_bank[j], t, g, comm_codes[h, g][:].bitcast(FP8X4), comm_plane[h, g][:], g == 0, False)
 
         def home_passes(j):
             h, t = divmod(j, TILES)
             for g in range(2):
-                codes, scales = x_operand(t, g)
-                nc.tensor.matmul_mx(
-                    out=sum_bank[j][:], lhsT=codes, lhsT_scale=scales,
-                    rhs=hw[h][:, g, :].bitcast(FP4X4), rhs_scale=hs[:, g, W * h : W * (h + 1)],
-                    start=False, stop=(g == 1),
+                mx_pass(
+                    sum_bank[j], t, g, home_codes[h][:, g, :].bitcast(FP4X4),
+                    home_plane[:, g, W * h : W * (h + 1)], False, g == 1,
                 )
 
         open_cols = sb("open_cols", [P, TILES], F32)
-        exposure, y, ybf = {}, {}, {}
-        halves = (slice(0, W // 2), slice(W // 2, W))
+        exposure, y, rounded = {}, {}, {}
+        col_halves = (slice(0, W // 2), slice(W // 2, W))
 
         def add_up(j):
             t = j % TILES
-            exposure[j] = sb("exposure%d" % j, [P, W], F32, tag="exposure%d" % (j % 3))
-            for cols in halves:
+            exposure[j] = sb("exposure%d" % j, [P, W], F32, tag="exposure%d" % (j % EXPOSURE_TILES))
+            for cols in col_halves:
                 nc.vector.scalar_tensor_tensor(
-                    out=exposure[j][:, cols], in0=work_sb[j][:, cols], scalar=open_cols[:, t : t + 1],
+                    out=exposure[j][:, cols], in0=work_out[j][:, cols], scalar=open_cols[:, t : t + 1],
                     in1=sum_bank[j][:, cols], op0=MULT, op1=ADD,
                 )
 
         def times_left(j, pieces):
             h, t = divmod(j, TILES)
-            y[j] = sb("y%d" % j, [P, W], F32, tag="y%d" % (j % 12))
+            y[j] = sb("y%d" % j, [P, W], F32)
             for cols in pieces:
                 nc.vector.tensor_tensor(
                     out=y[j][:, cols], in0=exposure[j][:, cols], in1=left_of[j][:, cols], op=MULT
                 )
             nc.sync.dma_start(out=out_0[P * t : P * (t + 1), W * h : W * (h + 1)], in_=y[j][:])
 
-        def new_ybf(j):
-            ybf[j] = sb("ybf%d" % j, [P, W], BF16, tag="ybf%d" % (j % 8))
-            return ybf[j][:].rearrange("b (u p e) -> b u p e", u=2, e=2)
+        def new_rounded(j):
+            rounded[j] = sb("rounded%d" % j, [P, W], BF16, tag="rounded%d" % (j % ROUNDED_TILES))
+            return rounded[j][:].rearrange("b (u p e) -> b u p e", u=2, e=2)
 
         def round_y(j):
-            nc.scalar.copy(out=new_ybf(j), in_=y[j][:].rearrange("b (p u e) -> b u p e", u=2, e=2))
+            nc.scalar.copy(out=new_rounded(j), in_=y[j][:].rearrange("b (p u e) -> b u p e", u=2, e=2))
 
         def times_left_rounded(j):
-            sorted_out = new_ybf(j)
-            for k in range(2):
+            places = new_rounded(j)
+            for k, cols in enumerate(col_halves):
                 nc.vector.tensor_tensor(
-                    out=sorted_out[:, :, 64 * k : 64 * (k + 1), :],
-                    in0=exposure[j][:, halves[k]].rearrange("b (p u e) -> b u p e", u=2, e=2),
-                    in1=left_of[j][:, halves[k]].rearrange("b (p u e) -> b u p e", u=2, e=2),
+                    out=places[:, :, P // 2 * k : P // 2 * (k + 1), :],
+                    in0=exposure[j][:, cols].rearrange("b (p u e) -> b u p e", u=2, e=2),
+                    in1=left_of[j][:, cols].rearrange("b (p u e) -> b u p e", u=2, e=2),
                     op=MULT,
                 )
 
-        turn_bank, turned = {}, {}
+        turn_bank, turned, out_codes = {}, {}, {}
 
         def turn(j, count):
-            turn_bank[j] = new_bank()
-            view = turn_bank[j][:, : 2 * P * count].rearrange("p (u m) -> p u m", u=2)
+            turn_bank[j] = new_bank("short", SHORT_BANKS)
+            by_u = turn_bank[j][:, : 2 * P * count].rearrange("p (u m) -> p u m", u=2)
             for k in range(count):
-                words = ybf[j + k][:].bitcast(F32)
+                pairs = rounded[j + k][:].bitcast(F32)
                 for u in range(2):
-                    nc.tensor.transpose(view[:, u, P * k : P * (k + 1)], words[:, P * u : P * (u + 1)], ident[:])
+                    nc.tensor.transpose(by_u[:, u, P * k : P * (k + 1)], pairs[:, P * u : P * (u + 1)], ident[:])
 
         def turn_copy(j, count):
-            turned[j] = sb("turned%d" % j, [P, 4 * P * count], BF16, tag="turned%d" % ((j // 2 + j % 2) % 3))
+            n = len(turned)
+            turned[j] = sb("turned%d" % j, [P, 4 * P * count], BF16, tag="turned%d" % (n % TURNED_TILES))
             nc.scalar.copy(
                 out=turned[j][:].bitcast(F32).rearrange("p (m u) -> p m u", u=2),
                 in_=turn_bank[j][:, : 2 * P * count].rearrange("p (u m) -> p m u", u=2),
             )
 
-        early_scales = sb("early_scales", [P, 2, EARLY_COLS], U8)
-        late_scales = sb("late_scales", [P, 2, M - EARLY_COLS], U8)
-
-        pair_codes = {}
+        early_plane = sb("early_plane", [P, 2, EARLY_COLS], U8)
+        late_plane = sb("late_plane", [P, 2, M - EARLY_COLS], U8)
 
         def quantize_y(j, count):
             h, t = divmod(j, TILES)
-            pair = j // 2
-            if j % 2 == 0:
-                pair_codes[pair] = sb("codes%d" % pair, [P, 2 * P], U32, tag="codes%d" % (pair % 4))
-            codes = pair_codes[pair]
+            first, end = [run for run in CODE_STORES if run[0] <= j < run[1]][0]
+            if j == first:
+                out_codes[first] = sb("out_codes%d" % first, [P, P * (end - first)], U32)
             c0, c1 = P * t, P * (t + count)
             if c0 < EARLY_COLS:
-                scales = early_scales[:, h, c0:c1]
+                scales = early_plane[:, h, c0:c1]
             else:
-                scales = late_scales[:, h, c0 - EARLY_COLS : c1 - EARLY_COLS]
-            w0 = P * (j % 2)
+                scales = late_plane[:, h, c0 - EARLY_COLS : c1 - EARLY_COLS]
+            w0 = P * (j - first)
             nc.vector.quantize_mx(
-                out=codes[:, w0 : w0 + P * count].bitcast(FP8X4), scales=scales, in_=turned[j][:]
+                out=out_codes[first][:, w0 : w0 + P * count].bitcast(FP8X4), scales=scales, in_=turned[j][:]
             )
-            if (j + count) % 2 == 0:
+            if j + count == end:
                 nc.sync.dma_start(
-                    out=out_1[h].rearrange("p m t -> p (m t)")[:, 4 * (c1 - 2 * P) : 4 * c1].bitcast(I32),
-                    in_=codes[:].bitcast(I32),
+                    out=out_1[h].rearrange("p m t -> p (m t)")[:, 4 * P * (first % TILES) : 4 * c1].bitcast(I32),
+                    in_=out_codes[first][:].bitcast(I32),
                 )
 
         def store_scales(engine, plane, c0, c1, quadrant):
@@ -298,52 +299,62 @@ def tile_vaccinated_generation_step_k3_kernel(
         for g in range(2):
             interleave_comm(0, g)
             quantize_comm(0, g)
-        for j in range(HEAD):
+        for j in range(HEAD_UNITS):
             comm_pass(j, 0)
-        open_bank = new_bank()
-        nc.tensor.transpose(open_bank[:, :P], open_rows32[:], ident[:])
+        open_bank = new_bank("short", SHORT_BANKS)
+        nc.tensor.transpose(open_bank[:, :P], open_square[:], ident[:])
         nc.scalar.copy(out=open_cols[:], in_=open_bank[:, :TILES])
-        for j in range(HEAD):
+        for j in range(HEAD_UNITS):
             comm_pass(j, 1)
+        for j in range(HEAD_HOME_UNITS):
+            home_passes(j)
+        work_passes(0)
+        work_copy(0)
 
-        turn_runs = {7: (0, 2, 4), 13: (6, 8, 10), 17: (12, 14)}
+        units_rounded = 0
         for s in range(UNITS):
-            work_passes(s)
-            if s >= HEAD:
+            turned_last_step = TURN_RUNS.get(s - 1, ())
+            if s < LAST:
+                work_passes(s + 1)
+            if s >= HEAD_UNITS:
                 comm_pass(s, 0)
                 comm_pass(s, 1)
-            home_passes(s)
-            for j in turn_runs.get(s - 1, ()):
+            if s >= HEAD_HOME_UNITS:
+                home_passes(s)
+            for j in turned_last_step:
                 turn_copy(j, 2)
-            work_copy(s)
+            if s < LAST:
+                work_copy(s + 1)
             if s >= 1:
                 add_up(s - 1)
-                times_left(s - 1, halves)
-                round_y(s - 1)
-            if s in (4, 6):
-                interleave_comm(1, (s - 4) // 2)
-            if s in (5, 7):
-                quantize_comm(1, (s - 5) // 2)
-            for j in turn_runs.get(s - 1, ()):
+                times_left(s - 1, col_halves)
+            round_until = s if s >= CATCH_UP_STEP else max(s - 1, 0)
+            for j in range(units_rounded, round_until):
+                round_y(j)
+            units_rounded = round_until
+            if s in SECOND_HALF_STEPS:
+                interleave_comm(1, SECOND_HALF_STEPS.index(s))
+            if s - 1 in SECOND_HALF_STEPS:
+                quantize_comm(1, SECOND_HALF_STEPS.index(s - 1))
+            for j in turned_last_step:
                 quantize_y(j, 2)
-            if s - 1 == 17:
+            if s - 1 == max(TURN_RUNS):
                 for q in range(4):
-                    store_scales(nc.sync, early_scales, 0, EARLY_COLS, q)
-            for j in turn_runs.get(s, ()):
+                    store_scales(nc.sync, early_plane, 0, EARLY_COLS, q)
+            for j in TURN_RUNS.get(s, ()):
                 turn(j, 2)
 
-        last = UNITS - 1
-        turn(last - 3, 2)
-        turn(last - 1, 1)
-        turn_copy(last - 3, 2)
-        turn_copy(last - 1, 1)
-        add_up(last)
-        times_left_rounded(last)
-        turn(last, 1)
-        turn_copy(last, 1)
-        times_left(last, (slice(0, W),))
-        quantize_y(last - 3, 2)
-        quantize_y(last - 1, 1)
-        quantize_y(last, 1)
+        turn(LAST - 3, 2)
+        turn_copy(LAST - 3, 2)
+        turn(LAST - 1, 1)
+        turn_copy(LAST - 1, 1)
+        add_up(LAST)
+        times_left_rounded(LAST)
+        turn(LAST, 1)
+        turn_copy(LAST, 1)
+        times_left(LAST, (slice(0, W),))
+        quantize_y(LAST - 3, 2)
+        quantize_y(LAST - 1, 1)
+        quantize_y(LAST, 1)
         for q in range(4):
-            store_scales(nc.sync if q < 2 else nc.scalar, late_scales, EARLY_COLS, M, q)
+            store_scales(nc.sync if q < 2 else nc.scalar, late_plane, EARLY_COLS, M, q)

from contextlib import ExitStack

import concourse.mybir as mybir
from concourse.masks import make_identity

F32 = mybir.dt.float32
BF16 = mybir.dt.bfloat16
I32 = mybir.dt.int32
U32 = mybir.dt.uint32
U8 = mybir.dt.uint8
FP8X4 = mybir.dt.float8_e4m3fn_x4
FP4X4 = mybir.dt.float4_e2m1fn_x4
ADD = mybir.AluOpType.add
MULT = mybir.AluOpType.mult

M, N = 1280, 1024
FLOPS = 3 * 2 * M * N * N

P = 128
W = 512
TILES = M // P
UNITS = 2 * TILES
LAST = UNITS - 1

SUM_BANKS = 4
SHORT_BANKS = 4
HEAD_UNITS = SUM_BANKS
HEAD_HOME_UNITS = 2

VECTOR_COLS = 352
SECOND_HALF_STEPS = (5, 7)

X_LOADS = ((0, 256), (256, 512), (512, 896), (896, 1280))
LEFT_LOADS = ((0, 0, 2), (0, 2, 6), (0, 6, 10), (1, 0, 5), (1, 5, 10))
WORK_SHIFT = 4

TURN_RUNS = {8: (0, 2, 4), 14: (6, 8, 10), 17: (12, 14)}
CATCH_UP_STEP = 16
CODE_STORES = ((0, 6), (6, 10), (10, 12), (12, 16), (16, 18), (18, 20))
EARLY_COLS = 768

WORK_TILES, EXPOSURE_TILES, ROUNDED_TILES, TURNED_TILES = 6, 3, 8, 3


def tile_vaccinated_generation_step_k3_kernel(
    tc, x_words, x_scales, home_words, home_scales, work_words, work_scales, comm, open_work, left,
    out_0, out_1, out_2,
):
    nc = tc.nc
    with ExitStack() as ctx:
        keep = ctx.enter_context(tc.tile_pool(name="keep", bufs=1))
        psum = ctx.enter_context(tc.psum_pool(name="psum", bufs=1))
        ctx.enter_context(tc.manual_schedule())

        def sb(name, shape, dtype, tag=None):
            return keep.tile(shape, dtype, name=name, tag=tag or name, align_bytes=64)

        banks_taken = {"sum": 0, "short": 0}

        def new_bank(kind, count):
            n = banks_taken[kind]
            banks_taken[kind] = n + 1
            return psum.tile([P, W], F32, name="%s%d" % (kind, n), tag="%s%d" % (kind, n % count))

        x_plane = sb("x_plane", [P, 2, M], U8)
        work_plane = sb("work_plane", [P, 2, N], U8)
        home_plane = sb("home_plane", [P, 2, N], U8)
        nc.vector.memset(x_plane[:].bitcast(I32), 0)
        nc.vector.memset(home_plane[:].bitcast(I32), 0)
        nc.vector.memset(work_plane[:].bitcast(I32), 0)

        open_rows = sb("open_rows", [TILES, P], BF16)
        nc.gpsimd.dma_start(out=open_rows[:], in_=open_work.rearrange("(t p) -> t p", p=P))
        open_square = sb("open_square", [P, P], F32)
        nc.gpsimd.memset(open_square[:], 0.0)
        ident = sb("ident", [P, P], F32)
        make_identity(nc, ident[:])
        nc.gpsimd.tensor_copy(out=open_square[:TILES, :], in_=open_rows[:])

        def load_scales(engine, plane, scales, quadrant, shift):
            p0 = 32 * quadrant + shift
            engine.dma_start(
                out=plane[p0 : p0 + 4, :, :].bitcast(I32),
                in_=scales[:, 4 * quadrant : 4 * quadrant + 4, :].rearrange("g r n -> r g n").bitcast(I32),
            )

        x_codes, work_codes, home_codes, comm_rows, left_of = {}, {}, {}, {}, {}

        def load_x(c):
            c0, c1 = X_LOADS[c]
            x_codes[c] = sb("x_codes%d" % c, [P, 2, c1 - c0], U32)
            nc.sync.dma_start(
                out=x_codes[c][:].bitcast(I32),
                in_=x_words.rearrange("g p n t -> p g (n t)")[:, :, 4 * c0 : 4 * c1].bitcast(I32),
            )

        def load_work(h):
            work_codes[h] = sb("work_codes%d" % h, [P, 2, W], U32)
            nc.sync.dma_start(
                out=work_codes[h][:].bitcast(I32),
                in_=work_words.rearrange("g p n t -> p g (n t)")[:, :, 4 * W * h : 4 * W * (h + 1)].bitcast(I32),
            )

        def load_home(h):
            home_codes[h] = sb("home_codes%d" % h, [P, 2, 2 * W], U8)
            nc.sync.dma_start(
                out=home_codes[h][:].bitcast(I32),
                in_=home_words.rearrange("g p n -> p g n")[:, :, 2 * W * h : 2 * W * (h + 1)].bitcast(I32),
            )

        def load_comm(h, g):
            comm_rows[h, g] = sb("comm_rows%d%d" % (h, g), [P, 4, W], BF16)
            nc.sync.dma_start(
                out=comm_rows[h, g][:],
                in_=comm[W * g : W * (g + 1), W * h : W * (h + 1)].rearrange("(p t) n -> p t n", t=4),
            )

        def load_left(c):
            h, t0, t1 = LEFT_LOADS[c]
            rows = sb("left%d" % c, [P, t1 - t0, W], BF16)
            nc.sync.dma_start(
                out=rows[:],
                in_=left[P * t0 : P * t1, W * h : W * (h + 1)].rearrange("(t p) n -> p t n", p=P),
            )
            for t in range(t0, t1):
                left_of[TILES * h + t] = rows[:, t - t0, :]

        load_comm(0, 0)
        for q in range(2):
            load_scales(nc.scalar, x_plane, x_scales, q, 0)
        load_x(0)
        for q in range(2, 4):
            load_scales(nc.sync, x_plane, x_scales, q, 0)
        load_comm(0, 1)
        load_x(1)
        load_home(0)
        for q in range(4):
            load_scales(nc.sync, home_plane, home_scales, q, 0)
        load_work(0)
        for q in range(4):
            load_scales(nc.sync, work_plane, work_scales, q, WORK_SHIFT)
        load_left(0)
        load_x(2)
        load_left(1)
        load_comm(1, 0)
        load_x(3)
        load_comm(1, 1)
        load_left(2)
        load_work(1)
        load_home(1)
        load_left(3)
        load_left(4)

        comm_grouped, comm_codes, comm_plane = {}, {}, {}

        def interleave_comm(h, g):
            comm_grouped[h, g] = sb("comm_grouped%d%d" % (h, g), [P, W, 4], BF16)
            by_column = comm_rows[h, g][:].rearrange("p t n -> p n t")
            nc.vector.tensor_copy(out=comm_grouped[h, g][:, :VECTOR_COLS, :], in_=by_column[:, :VECTOR_COLS, :])
            nc.scalar.copy(out=comm_grouped[h, g][:, VECTOR_COLS:, :], in_=by_column[:, VECTOR_COLS:, :])

        def quantize_comm(h, g):
            comm_codes[h, g] = sb("comm_codes%d%d" % (h, g), [P, W], U32)
            comm_plane[h, g] = sb("comm_plane%d%d" % (h, g), [P, W], U8)
            nc.vector.quantize_mx(
                out=comm_codes[h, g][:].bitcast(FP8X4),
                scales=comm_plane[h, g][:],
                in_=comm_grouped[h, g][:].rearrange("p n t -> p (n t)"),
            )

        work_bank, work_out, sum_bank = {}, {}, {}

        def mx_pass(bank, t, g, codes, plane, start, stop):
            c = [k for k, (c0, c1) in enumerate(X_LOADS) if c0 <= P * t < c1][0]
            w0 = P * t - X_LOADS[c][0]
            nc.tensor.matmul_mx(
                out=bank[:],
                lhsT=x_codes[c][:, g, w0 : w0 + P].bitcast(FP8X4),
                lhsT_scale=x_plane[:, g, P * t : P * (t + 1)],
                rhs=codes,
                rhs_scale=plane,
                start=start,
                stop=stop,
            )

        def work_passes(j):
            h, t = divmod(j, TILES)
            work_bank[j] = new_bank("short", SHORT_BANKS)
            for g in range(2):
                mx_pass(
                    work_bank[j], t, g, work_codes[h][:, g, :].bitcast(FP8X4),
                    work_plane[WORK_SHIFT:, g, W * h : W * (h + 1)], g == 0, g == 1,
                )

        def work_copy(j):
            work_out[j] = sb("work_out%d" % j, [P, W], F32, tag="work_out%d" % (j % WORK_TILES))
            nc.scalar.copy(out=work_out[j][:], in_=work_bank[j][:])

        def comm_pass(j, g):
            h, t = divmod(j, TILES)
            if g == 0:
                sum_bank[j] = new_bank("sum", SUM_BANKS)
            mx_pass(sum_bank[j], t, g, comm_codes[h, g][:].bitcast(FP8X4), comm_plane[h, g][:], g == 0, False)

        def home_passes(j):
            h, t = divmod(j, TILES)
            for g in range(2):
                mx_pass(
                    sum_bank[j], t, g, home_codes[h][:, g, :].bitcast(FP4X4),
                    home_plane[:, g, W * h : W * (h + 1)], False, g == 1,
                )

        open_cols = sb("open_cols", [P, TILES], F32)
        exposure, y, rounded = {}, {}, {}
        col_halves = (slice(0, W // 2), slice(W // 2, W))

        def add_up(j):
            t = j % TILES
            exposure[j] = sb("exposure%d" % j, [P, W], F32, tag="exposure%d" % (j % EXPOSURE_TILES))
            for cols in col_halves:
                nc.vector.scalar_tensor_tensor(
                    out=exposure[j][:, cols], in0=work_out[j][:, cols], scalar=open_cols[:, t : t + 1],
                    in1=sum_bank[j][:, cols], op0=MULT, op1=ADD,
                )

        def times_left(j, pieces):
            h, t = divmod(j, TILES)
            y[j] = sb("y%d" % j, [P, W], F32)
            for cols in pieces:
                nc.vector.tensor_tensor(
                    out=y[j][:, cols], in0=exposure[j][:, cols], in1=left_of[j][:, cols], op=MULT
                )
            nc.sync.dma_start(out=out_0[P * t : P * (t + 1), W * h : W * (h + 1)], in_=y[j][:])

        def new_rounded(j):
            rounded[j] = sb("rounded%d" % j, [P, W], BF16, tag="rounded%d" % (j % ROUNDED_TILES))
            return rounded[j][:].rearrange("b (u p e) -> b u p e", u=2, e=2)

        def round_y(j):
            nc.scalar.copy(out=new_rounded(j), in_=y[j][:].rearrange("b (p u e) -> b u p e", u=2, e=2))

        def times_left_rounded(j):
            places = new_rounded(j)
            for k, cols in enumerate(col_halves):
                nc.vector.tensor_tensor(
                    out=places[:, :, P // 2 * k : P // 2 * (k + 1), :],
                    in0=exposure[j][:, cols].rearrange("b (p u e) -> b u p e", u=2, e=2),
                    in1=left_of[j][:, cols].rearrange("b (p u e) -> b u p e", u=2, e=2),
                    op=MULT,
                )

        turn_bank, turned, out_codes = {}, {}, {}

        def turn(j, count):
            turn_bank[j] = new_bank("short", SHORT_BANKS)
            by_u = turn_bank[j][:, : 2 * P * count].rearrange("p (u m) -> p u m", u=2)
            for k in range(count):
                pairs = rounded[j + k][:].bitcast(F32)
                for u in range(2):
                    nc.tensor.transpose(by_u[:, u, P * k : P * (k + 1)], pairs[:, P * u : P * (u + 1)], ident[:])

        def turn_copy(j, count):
            n = len(turned)
            turned[j] = sb("turned%d" % j, [P, 4 * P * count], BF16, tag="turned%d" % (n % TURNED_TILES))
            nc.scalar.copy(
                out=turned[j][:].bitcast(F32).rearrange("p (m u) -> p m u", u=2),
                in_=turn_bank[j][:, : 2 * P * count].rearrange("p (u m) -> p m u", u=2),
            )

        early_plane = sb("early_plane", [P, 2, EARLY_COLS], U8)
        late_plane = sb("late_plane", [P, 2, M - EARLY_COLS], U8)

        def quantize_y(j, count):
            h, t = divmod(j, TILES)
            first, end = [run for run in CODE_STORES if run[0] <= j < run[1]][0]
            if j == first:
                out_codes[first] = sb("out_codes%d" % first, [P, P * (end - first)], U32)
            c0, c1 = P * t, P * (t + count)
            if c0 < EARLY_COLS:
                scales = early_plane[:, h, c0:c1]
            else:
                scales = late_plane[:, h, c0 - EARLY_COLS : c1 - EARLY_COLS]
            w0 = P * (j - first)
            nc.vector.quantize_mx(
                out=out_codes[first][:, w0 : w0 + P * count].bitcast(FP8X4), scales=scales, in_=turned[j][:]
            )
            if j + count == end:
                nc.sync.dma_start(
                    out=out_1[h].rearrange("p m t -> p (m t)")[:, 4 * P * (first % TILES) : 4 * c1].bitcast(I32),
                    in_=out_codes[first][:].bitcast(I32),
                )

        def store_scales(engine, plane, c0, c1, quadrant):
            engine.dma_start(
                out=out_2[:, 4 * quadrant : 4 * quadrant + 4, c0:c1].rearrange("g r m -> r g m").bitcast(I32),
                in_=plane[32 * quadrant : 32 * quadrant + 4, :, :].bitcast(I32),
            )

        for g in range(2):
            interleave_comm(0, g)
            quantize_comm(0, g)
        for j in range(HEAD_UNITS):
            comm_pass(j, 0)
        open_bank = new_bank("short", SHORT_BANKS)
        nc.tensor.transpose(open_bank[:, :P], open_square[:], ident[:])
        nc.scalar.copy(out=open_cols[:], in_=open_bank[:, :TILES])
        for j in range(HEAD_UNITS):
            comm_pass(j, 1)
        for j in range(HEAD_HOME_UNITS):
            home_passes(j)
        work_passes(0)
        work_copy(0)

        units_rounded = 0
        for s in range(UNITS):
            turned_last_step = TURN_RUNS.get(s - 1, ())
            if s < LAST:
                work_passes(s + 1)
            if s >= HEAD_UNITS:
                comm_pass(s, 0)
                comm_pass(s, 1)
            if s >= HEAD_HOME_UNITS:
                home_passes(s)
            for j in turned_last_step:
                turn_copy(j, 2)
            if s < LAST:
                work_copy(s + 1)
            if s >= 1:
                add_up(s - 1)
                times_left(s - 1, col_halves)
            round_until = s if s >= CATCH_UP_STEP else max(s - 1, 0)
            for j in range(units_rounded, round_until):
                round_y(j)
            units_rounded = round_until
            if s in SECOND_HALF_STEPS:
                interleave_comm(1, SECOND_HALF_STEPS.index(s))
            if s - 1 in SECOND_HALF_STEPS:
                quantize_comm(1, SECOND_HALF_STEPS.index(s - 1))
            for j in turned_last_step:
                quantize_y(j, 2)
            if s - 1 == max(TURN_RUNS):
                for q in range(4):
                    store_scales(nc.sync, early_plane, 0, EARLY_COLS, q)
            for j in TURN_RUNS.get(s, ()):
                turn(j, 2)

        turn(LAST - 3, 2)
        turn_copy(LAST - 3, 2)
        turn(LAST - 1, 1)
        turn_copy(LAST - 1, 1)
        add_up(LAST)
        times_left_rounded(LAST)
        turn(LAST, 1)
        turn_copy(LAST, 1)
        times_left(LAST, (slice(0, W),))
        quantize_y(LAST - 3, 2)
        quantize_y(LAST - 1, 1)
        quantize_y(LAST, 1)
        for q in range(4):
            store_scales(nc.sync if q < 2 else nc.scalar, late_plane, EARLY_COLS, M, q)
